import numpy as np
import ml_dtypes


def mxq(x, axis, fmt="e4m3"):
    dtype, down = {"e4m3": (ml_dtypes.float8_e4m3fn, 7), "e5m2": (ml_dtypes.float8_e5m2, 14)}[fmt]
    v = np.moveaxis(np.asarray(x, np.float32).astype(ml_dtypes.bfloat16).astype(np.float64), axis, -1)
    blocks = v.reshape(v.shape[:-1] + (-1, 32))
    amax = np.abs(blocks).max(-1, keepdims=True)
    byte = np.maximum(np.where(amax > 0, np.frexp(amax)[1] - 1 + 127, 0) - down, 1)
    scale = np.exp2(byte - 127.0)
    codes = (blocks / scale).astype(np.float32).astype(dtype).astype(np.float64)
    return np.moveaxis((codes * scale).reshape(v.shape), -1, axis)


WIDE = False


def mx_kscale(k):
    if not WIDE:
        return np.ones(k)
    levels = np.array([10, -10, 5, -5, 0])
    if k % 512:
        return np.exp2(np.random.permutation(np.resize(levels, k // 32))).repeat(32)
    a = np.empty((k // 512, 16))
    for p in range(k // 512):
        a[p, :8] = np.random.permutation(np.resize(levels, 8))
        for g in range(8):
            far = levels[np.abs(levels - a[p, g]) >= 10]
            a[p, g + 8] = far[np.random.randint(len(far))]
    return np.exp2(a.ravel()).repeat(32)


def f64(x):
    return np.asarray(x).astype(np.float64)


def striped8(idx):
    return np.concatenate([v.reshape(-1, 16).T for v in idx]).astype(np.uint16)


def unstriped8(offs):
    return np.stack([offs[16 * g:16 * g + 16].T.reshape(-1) for g in range(8)]).astype(np.int64)


def split(x):
    m, e = np.frexp(f64(x))
    hi = np.ldexp(np.trunc(16.0 * m) / 16.0, e)
    return hi, f64(x) - hi


def gelu(v):
    return 0.5 * v * (1.0 + np.tanh(np.sqrt(2.0 / np.pi) * (v + 0.044715 * v**3)))


K, M, T, S = 1024, 512, 1024, 512


def setup_inputs():
    n = np.random.standard_normal
    s = mx_kscale(K)[:, None]
    return {
        "xT": (n((K, T)) * s).astype(np.float32),
        "w": (n((K, M)) / np.sqrt(K) / s).astype(np.float32),
        "wgt": np.repeat(np.random.uniform(0.5, 2.0, (8, S)), 16, axis=0).astype(np.float32),
        "b": (0.3 * n(512)).astype(np.float32),
        "offs": striped8(np.stack([np.random.permutation(T)[:S] for _ in range(8)])),
    }


def reference(xT, w, wgt, b, offs):
    idx = unstriped8(offs)
    group = np.arange(K) % 512 // 64
    xg = f64(wgt)[np.arange(K) // 4 % 128] * f64(xT)[np.arange(K)[:, None], idx[group]]
    xT_ = mxq(xg, 0, "e4m3")
    w_hi, w_lo = split(w)
    w_hi_, w_lo_ = mxq(w_hi, 0, "e4m3"), mxq(w_lo, 0, "e4m3")
    y = xT_.T @ w_hi_ + xT_.T @ w_lo_
    return gelu(y + f64(b)[None, :])

@@ -1,0 +1,217 @@
+from contextlib import ExitStack
+
+import concourse.mybir as mybir
+
+K, M, T, S = 1024, 512, 1024, 512
+FLOPS = 2 * 2 * K * M * S
+
+F32 = mybir.dt.float32
+BF16 = mybir.dt.bfloat16
+I32 = mybir.dt.int32
+U32 = mybir.dt.uint32
+U16 = mybir.dt.uint16
+U8 = mybir.dt.uint8
+FP8X4 = mybir.dt.float8_e4m3fn_x4
+ALU = mybir.AluOpType
+ACT = mybir.ActivationFunctionType
+
+P = 128
+PACK = 4
+PASSES = K // (P * PACK)
+HALF = 256
+PIECES = (((0, 128), (128, 256), (256, 512)), ((0, 256), (256, 512)))
+CUTS = (((0, 512),), ((0, 512),), ((0, 512),), ((0, 256), (256, 512)))
+HI_MASK = -0x000F0010
+
+
+def four_by_four(view):
+    return view.rearrange("p j (c i) -> p c j i", i=4)
+
+
+def packed(view):
+    return view.rearrange("p (c i) j -> p c j i", i=4)
+
+
+def tile_list_heads_tm_hl_gelu_kernel(tc, xT, w, wgt, b, offs, out):
+    nc = tc.nc
+    with ExitStack() as ctx:
+        keep = ctx.enter_context(tc.tile_pool(name="keep", bufs=1))
+        psum = ctx.enter_context(tc.psum_pool(name="psum", bufs=1))
+
+        offsets = keep.tile([P, S // 16], U16, name="offsets")
+        weights = keep.tile([P, S], F32, name="weights")
+        bias = keep.tile([P, M], F32, name="bias")
+        planes = [[keep.tile([P, T], F32, name=f"x{a}{i}") for i in range(PACK)] for a in range(PASSES)]
+        w_raw = [
+            [keep.tile([P, PACK, n1 - n0], F32, name=f"w{a}_{n0}") for n0, n1 in PIECES[a]] for a in range(PASSES)
+        ]
+        warm = keep.tile([P, 2], F32, name="warm")
+        w_hi = [keep.tile([P, M, PACK], BF16, name=f"whi{a}", align_bytes=64) for a in range(PASSES)]
+        w_lo = [keep.tile([P, M, PACK], BF16, name=f"wlo{a}", align_bytes=64) for a in range(PASSES)]
+        hi_codes = [keep.tile([P, M], U32, name=f"hic{a}", align_bytes=64) for a in range(PASSES)]
+        lo_codes = [keep.tile([P, M], U32, name=f"loc{a}", align_bytes=64) for a in range(PASSES)]
+        hi_scales = [keep.tile([P, M], U8, name=f"his{a}", align_bytes=64) for a in range(PASSES)]
+        lo_scales = [keep.tile([P, M], U8, name=f"los{a}", align_bytes=64) for a in range(PASSES)]
+        picked = [[keep.tile([P, PACK, HALF], F32, name=f"g{a}{h}") for h in range(2)] for a in range(PASSES)]
+        xg = [[keep.tile([P, HALF, PACK], BF16, name=f"xg{a}{h}", align_bytes=64) for h in range(2)] for a in range(PASSES)]
+        x_codes = [[keep.tile([P, HALF], U32, name=f"xc{a}{h}", align_bytes=64) for h in range(2)] for a in range(PASSES)]
+        x_scales = [[keep.tile([P, HALF], U8, name=f"xs{a}{h}", align_bytes=64) for h in range(2)] for a in range(PASSES)]
+        acc = [
+            [(psum.tile([P, n1 - n0], F32, name=f"acc{m}_{n0}"), n0, n1) for n0, n1 in cuts]
+            for m, cuts in enumerate(CUTS)
+        ]
+
+        xv = xT.rearrange("(a p j) t -> a j p t", a=PASSES, j=PACK)
+        wv = w.rearrange("(a p j) n -> a p j n", a=PASSES, j=PACK)
+
+        nc.gpsimd.memset(warm[:, 0:1], 0.0)
+        nc.scalar.activation(warm[:, 1:2], warm[:, 0:1], ACT.Gelu_apprx_tanh)
+
+        def load_plane(a, i):
+            nc.sync.dma_start(out=planes[a][i][:], in_=xv[a, i])
+
+        def load_w(a, q):
+            n0, n1 = PIECES[a][q]
+            nc.sync.dma_start(out=w_raw[a][q][:], in_=wv[a, :, :, n0:n1])
+
+        nc.sync.dma_start(offsets[:], offs)
+        load_plane(0, 0)
+        nc.sync.dma_start(out=weights[:, 0:HALF], in_=wgt[:, 0:HALF])
+        nc.sync.dma_start(out=weights[:, HALF:S], in_=wgt[:, HALF:S])
+        load_plane(0, 1)
+        load_plane(0, 2)
+        load_w(0, 0)
+        load_plane(0, 3)
+        load_w(0, 1)
+        load_plane(1, 0)
+        load_w(0, 2)
+        load_w(1, 0)
+        load_w(1, 1)
+        for i in range(1, PACK):
+            load_plane(1, i)
+        nc.sync.dma_start(out=bias[:], in_=b.partition_broadcast(P))
+
+        def gather(a, i, t0, t1):
+            h, cols = t0 // HALF, slice(t0 % HALF, t0 % HALF + t1 - t0)
+            nc.vector.tensor_tensor(
+                picked[a][h][:, i, cols],
+                planes[a][i][:].indirect(offsets[:, t0 // 16 : t1 // 16]),
+                weights[:, t0:t1],
+                ALU.mult,
+            )
+
+        def interleave(a, t0, t1):
+            h, cols = t0 // HALF, slice(t0 % HALF, t0 % HALF + t1 - t0)
+            nc.scalar.copy(packed(xg[a][h][:, cols, :]), four_by_four(picked[a][h][:, :, cols]))
+
+        def quantize_x(a, t0, t1):
+            h, cols = t0 // HALF, slice(t0 % HALF, t0 % HALF + t1 - t0)
+            nc.vector.quantize_mx(
+                out=x_codes[a][h][:, cols].bitcast(FP8X4),
+                scales=x_scales[a][h][:, cols],
+                in_=xg[a][h][:, cols, :].rearrange("p t j -> p (t j)"),
+            )
+
+        def truncate(a, q):
+            n0, n1 = PIECES[a][q]
+            top = w_raw[a][q][:].bitcast(BF16).rearrange("p j (n e) -> p j n e", e=2)[:, :, :, 1]
+            nc.scalar.copy(packed(w_hi[a][:, n0:n1, :]), four_by_four(top))
+
+        def mask(a, q):
+            n0, n1 = PIECES[a][q]
+            words = w_hi[a][:, n0:n1, :].rearrange("p n j -> p (n j)").bitcast(I32)
+            nc.vector.tensor_scalar(words, words, HI_MASK, None, ALU.bitwise_and)
+
+        def rest(a, q):
+            cols = slice(*PIECES[a][q])
+            nc.vector.tensor_tensor(
+                packed(w_lo[a][:, cols, :]), four_by_four(w_raw[a][q][:]), packed(w_hi[a][:, cols, :]), ALU.subtract
+            )
+
+        def quantize_w(codes, scales, source):
+            nc.vector.quantize_mx(
+                out=codes[:].bitcast(FP8X4), scales=scales[:], in_=source[:].rearrange("p n j -> p (n j)")
+            )
+
+        def multiply(a, m, low):
+            h, cols = m // 2, slice((m % 2) * P, (m % 2) * P + P)
+            codes, scales = ((hi_codes[a], hi_scales[a]), (lo_codes[a], lo_scales[a]))[low]
+            for bank, n0, n1 in acc[m]:
+                nc.tensor.matmul_mx(
+                    out=bank[:],
+                    lhsT=x_codes[a][h][:, cols].bitcast(FP8X4),
+                    lhsT_scale=x_scales[a][h][:, cols],
+                    rhs=codes[:, n0:n1].bitcast(FP8X4),
+                    rhs_scale=scales[:, n0:n1],
+                    start=(a == 0 and low == 0),
+                    stop=(a == PASSES - 1 and low == 1),
+                )
+
+        def finish(m):
+            summed = keep.tile([P, M], F32, name=f"sum{m}")
+            result = keep.tile([P, M], F32, name=f"res{m}")
+            for bank, n0, n1 in acc[m]:
+                nc.vector.tensor_tensor(summed[:, n0:n1], bank[:], bias[:, n0:n1], ALU.add)
+                nc.scalar.activation(result[:, n0:n1], summed[:, n0:n1], ACT.Gelu_apprx_tanh)
+                nc.sync.dma_start(out=out[m * P : (m + 1) * P, n0:n1], in_=result[:, n0:n1])
+
+        for i in range(3):
+            gather(0, i, 0, 256)
+            gather(0, i, 256, 512)
+        truncate(0, 0)
+        mask(0, 0)
+        rest(0, 0)
+        gather(0, 3, 0, 256)
+        gather(0, 3, 256, 512)
+        truncate(0, 1)
+        mask(0, 1)
+        rest(0, 1)
+        truncate(0, 2)
+        interleave(0, 0, 256)
+        interleave(0, 256, 512)
+        quantize_x(0, 0, 256)
+        gather(1, 0, 0, 256)
+        gather(1, 0, 256, 384)
+        gather(1, 0, 384, 512)
+        mask(0, 2)
+        rest(0, 2)
+        quantize_w(hi_codes[0], hi_scales[0], w_hi[0])
+        truncate(1, 0)
+        quantize_x(0, 256, 512)
+        quantize_w(lo_codes[0], lo_scales[0], w_lo[0])
+        for m in range(4):
+            multiply(0, m, 0)
+        for m in range(4):
+            multiply(0, m, 1)
+        truncate(1, 1)
+        mask(1, 0)
+        rest(1, 0)
+        for i in range(1, PACK):
+            gather(1, i, 0, 256)
+        interleave(1, 0, 256)
+        mask(1, 1)
+        rest(1, 1)
+        quantize_w(hi_codes[1], hi_scales[1], w_hi[1])
+        quantize_x(1, 0, 256)
+        quantize_w(lo_codes[1], lo_scales[1], w_lo[1])
+        for m in range(2):
+            multiply(1, m, 0)
+        for m in range(2):
+            multiply(1, m, 1)
+        for i in range(1, PACK):
+            gather(1, i, 256, 384)
+        interleave(1, 256, 384)
+        gather(1, 1, 384, 512)
+        quantize_x(1, 256, 384)
+        gather(1, 2, 384, 512)
+        gather(1, 3, 384, 512)
+        interleave(1, 384, 512)
+        multiply(1, 2, 0)
+        multiply(1, 2, 1)
+        finish(0)
+        quantize_x(1, 384, 512)
+        finish(1)
+        multiply(1, 3, 0)
+        multiply(1, 3, 1)
+        finish(2)
+        finish(3)

@@ -19,7 +19,7 @@ P = 128
 PACK = 4
 PASSES = K // (P * PACK)
 HALF = 256
-PIECES = (((0, 128), (128, 256), (256, 512)), ((0, 256), (256, 512)))
+LOADS = (((0, 128), (128, 256), (256, 512)), ((0, 512),))
 CUTS = (((0, 512),), ((0, 512),), ((0, 512),), ((0, 256), (256, 512)))
 HI_MASK = -0x000F0010
 
@@ -43,7 +43,8 @@ def tile_list_heads_tm_hl_gelu_kernel(tc, xT, w, wgt, b, offs, out):
         bias = keep.tile([P, M], F32, name="bias")
         planes = [[keep.tile([P, T], F32, name=f"x{a}{i}") for i in range(PACK)] for a in range(PASSES)]
         w_raw = [
-            [keep.tile([P, PACK, n1 - n0], F32, name=f"w{a}_{n0}") for n0, n1 in PIECES[a]] for a in range(PASSES)
+            [(keep.tile([P, PACK, n1 - n0], F32, name=f"w{a}_{n0}"), n0, n1) for n0, n1 in LOADS[a]]
+            for a in range(PASSES)
         ]
         warm = keep.tile([P, 2], F32, name="warm")
         w_hi = [keep.tile([P, M, PACK], BF16, name=f"whi{a}", align_bytes=64) for a in range(PASSES)]
@@ -71,23 +72,25 @@ def tile_list_heads_tm_hl_gelu_kernel(tc, xT, w, wgt, b, offs, out):
             nc.sync.dma_start(out=planes[a][i][:], in_=xv[a, i])
 
         def load_w(a, q):
-            n0, n1 = PIECES[a][q]
-            nc.sync.dma_start(out=w_raw[a][q][:], in_=wv[a, :, :, n0:n1])
+            tile, n0, n1 = w_raw[a][q]
+            nc.sync.dma_start(out=tile[:], in_=wv[a, :, :, n0:n1])
 
-        nc.sync.dma_start(offsets[:], offs)
+        def w_part(a, n0, n1):
+            for tile, lo, hi in w_raw[a]:
+                if lo <= n0 and n1 <= hi:
+                    return tile[:, :, n0 - lo : n1 - lo]
+            raise ValueError("columns of two loads")
+
+        for q in range(3):
+            load_w(0, q)
         load_plane(0, 0)
-        nc.sync.dma_start(out=weights[:, 0:HALF], in_=wgt[:, 0:HALF])
-        nc.sync.dma_start(out=weights[:, HALF:S], in_=wgt[:, HALF:S])
+        nc.sync.dma_start(out=weights[:], in_=wgt)
+        nc.sync.dma_start(offsets[:], offs)
         load_plane(0, 1)
         load_plane(0, 2)
-        load_w(0, 0)
-        load_plane(0, 3)
-        load_w(0, 1)
-        load_plane(1, 0)
-        load_w(0, 2)
         load_w(1, 0)
-        load_w(1, 1)
-        for i in range(1, PACK):
+        load_plane(0, 3)
+        for i in range(PACK):
             load_plane(1, i)
         nc.sync.dma_start(out=bias[:], in_=b.partition_broadcast(P))
 
@@ -112,20 +115,20 @@ def tile_list_heads_tm_hl_gelu_kernel(tc, xT, w, wgt, b, offs, out):
                 in_=xg[a][h][:, cols, :].rearrange("p t j -> p (t j)"),
             )
 
-        def truncate(a, q):
-            n0, n1 = PIECES[a][q]
-            top = w_raw[a][q][:].bitcast(BF16).rearrange("p j (n e) -> p j n e", e=2)[:, :, :, 1]
-            nc.scalar.copy(packed(w_hi[a][:, n0:n1, :]), four_by_four(top))
+        def truncate(a, n0, n1, copy):
+            top = w_part(a, n0, n1).bitcast(BF16).rearrange("p j (n e) -> p j n e", e=2)[:, :, :, 1]
+            copy(packed(w_hi[a][:, n0:n1, :]), four_by_four(top))
 
-        def mask(a, q):
-            n0, n1 = PIECES[a][q]
+        def mask(a, n0, n1):
             words = w_hi[a][:, n0:n1, :].rearrange("p n j -> p (n j)").bitcast(I32)
             nc.vector.tensor_scalar(words, words, HI_MASK, None, ALU.bitwise_and)
 
-        def rest(a, q):
-            cols = slice(*PIECES[a][q])
+        def rest(a, n0, n1):
             nc.vector.tensor_tensor(
-                packed(w_lo[a][:, cols, :]), four_by_four(w_raw[a][q][:]), packed(w_hi[a][:, cols, :]), ALU.subtract
+                packed(w_lo[a][:, n0:n1, :]),
+                four_by_four(w_part(a, n0, n1)),
+                packed(w_hi[a][:, n0:n1, :]),
+                ALU.subtract,
             )
 
         def quantize_w(codes, scales, source):
@@ -155,63 +158,57 @@ def tile_list_heads_tm_hl_gelu_kernel(tc, xT, w, wgt, b, offs, out):
                 nc.scalar.activation(result[:, n0:n1], summed[:, n0:n1], ACT.Gelu_apprx_tanh)
                 nc.sync.dma_start(out=out[m * P : (m + 1) * P, n0:n1], in_=result[:, n0:n1])
 
+        truncate(0, 0, 128, nc.vector.tensor_copy)
+        for n0 in range(0, M, 128):
+            if n0:
+                truncate(0, n0, n0 + 128, nc.scalar.copy)
+            mask(0, n0, n0 + 128)
+            rest(0, n0, n0 + 128)
+        quantize_w(hi_codes[0], hi_scales[0], w_hi[0])
         for i in range(3):
             gather(0, i, 0, 256)
             gather(0, i, 256, 512)
-        truncate(0, 0)
-        mask(0, 0)
-        rest(0, 0)
+        quantize_w(lo_codes[0], lo_scales[0], w_lo[0])
+        for n0 in (0, 256):
+            truncate(1, n0, n0 + 256, nc.scalar.copy)
+        mask(1, 0, 256)
         gather(0, 3, 0, 256)
         gather(0, 3, 256, 512)
-        truncate(0, 1)
-        mask(0, 1)
-        rest(0, 1)
-        truncate(0, 2)
         interleave(0, 0, 256)
         interleave(0, 256, 512)
-        quantize_x(0, 0, 256)
+        rest(1, 0, 256)
         gather(1, 0, 0, 256)
-        gather(1, 0, 256, 384)
-        gather(1, 0, 384, 512)
-        mask(0, 2)
-        rest(0, 2)
-        quantize_w(hi_codes[0], hi_scales[0], w_hi[0])
-        truncate(1, 0)
+        mask(1, 256, 512)
+        quantize_x(0, 0, 256)
+        gather(1, 1, 0, 256)
         quantize_x(0, 256, 512)
-        quantize_w(lo_codes[0], lo_scales[0], w_lo[0])
-        for m in range(4):
-            multiply(0, m, 0)
-        for m in range(4):
-            multiply(0, m, 1)
-        truncate(1, 1)
-        mask(1, 0)
-        rest(1, 0)
-        for i in range(1, PACK):
-            gather(1, i, 0, 256)
+        for low in range(2):
+            for m in range(4):
+                multiply(0, m, low)
+        rest(1, 256, 512)
+        gather(1, 2, 0, 256)
+        gather(1, 3, 0, 256)
         interleave(1, 0, 256)
-        mask(1, 1)
-        rest(1, 1)
         quantize_w(hi_codes[1], hi_scales[1], w_hi[1])
+        gather(1, 0, 256, 384)
         quantize_x(1, 0, 256)
         quantize_w(lo_codes[1], lo_scales[1], w_lo[1])
         for m in range(2):
             multiply(1, m, 0)
-        for m in range(2):
             multiply(1, m, 1)
         for i in range(1, PACK):
             gather(1, i, 256, 384)
         interleave(1, 256, 384)
-        gather(1, 1, 384, 512)
-        quantize_x(1, 256, 384)
-        gather(1, 2, 384, 512)
-        gather(1, 3, 384, 512)
+        for i in range(PACK):
+            gather(1, i, 384, 512)
         interleave(1, 384, 512)
+        quantize_x(1, 256, 384)
         multiply(1, 2, 0)
         multiply(1, 2, 1)
         finish(0)
         quantize_x(1, 384, 512)
-        finish(1)
         multiply(1, 3, 0)
         multiply(1, 3, 1)
+        finish(1)
         finish(2)
         finish(3)

@@ -18,7 +18,7 @@ ACT = mybir.ActivationFunctionType
 P = 128
 PACK = 4
 PASSES = K // (P * PACK)
-HALF = 256
+HI, LO = 0, 1
 LOADS = (((0, 128), (128, 256), (256, 512)), ((0, 512),))
 CUTS = (((0, 512),), ((0, 512),), ((0, 512),), ((0, 256), (256, 512)))
 HI_MASK = -0x000F0010
@@ -41,22 +41,26 @@ def tile_list_heads_tm_hl_gelu_kernel(tc, xT, w, wgt, b, offs, out):
         offsets = keep.tile([P, S // 16], U16, name="offsets")
         weights = keep.tile([P, S], F32, name="weights")
         bias = keep.tile([P, M], F32, name="bias")
+        warm = keep.tile([P, 2], F32, name="warm")
         planes = [[keep.tile([P, T], F32, name=f"x{a}{i}") for i in range(PACK)] for a in range(PASSES)]
         w_raw = [
             [(keep.tile([P, PACK, n1 - n0], F32, name=f"w{a}_{n0}"), n0, n1) for n0, n1 in LOADS[a]]
             for a in range(PASSES)
         ]
-        warm = keep.tile([P, 2], F32, name="warm")
-        w_hi = [keep.tile([P, M, PACK], BF16, name=f"whi{a}", align_bytes=64) for a in range(PASSES)]
-        w_lo = [keep.tile([P, M, PACK], BF16, name=f"wlo{a}", align_bytes=64) for a in range(PASSES)]
-        hi_codes = [keep.tile([P, M], U32, name=f"hic{a}", align_bytes=64) for a in range(PASSES)]
-        lo_codes = [keep.tile([P, M], U32, name=f"loc{a}", align_bytes=64) for a in range(PASSES)]
-        hi_scales = [keep.tile([P, M], U8, name=f"his{a}", align_bytes=64) for a in range(PASSES)]
-        lo_scales = [keep.tile([P, M], U8, name=f"los{a}", align_bytes=64) for a in range(PASSES)]
-        picked = [[keep.tile([P, PACK, HALF], F32, name=f"g{a}{h}") for h in range(2)] for a in range(PASSES)]
-        xg = [[keep.tile([P, HALF, PACK], BF16, name=f"xg{a}{h}", align_bytes=64) for h in range(2)] for a in range(PASSES)]
-        x_codes = [[keep.tile([P, HALF], U32, name=f"xc{a}{h}", align_bytes=64) for h in range(2)] for a in range(PASSES)]
-        x_scales = [[keep.tile([P, HALF], U8, name=f"xs{a}{h}", align_bytes=64) for h in range(2)] for a in range(PASSES)]
+        split = [
+            keep.tile([P, 2, M, PACK], BF16, name="split0", align_bytes=64),
+            keep.tile([P, 2, M, PACK], BF16, name="split1", tag="shared", align_bytes=64),
+        ]
+        w_codes = [keep.tile([P, 2, M], U32, name=f"wc{a}", align_bytes=64) for a in range(PASSES)]
+        w_scales = [keep.tile([P, 2, M], U8, name=f"ws{a}", align_bytes=64) for a in range(PASSES)]
+        picked = {
+            (0, 0): keep.tile([P, PACK, 256], F32, name="g00"),
+            (0, 1): keep.tile([P, PACK, 256], F32, name="g01"),
+            (1, 0): keep.tile([P, PACK, 256], F32, name="g10"),
+        }
+        xg = [keep.tile([P, S, PACK], BF16, name=f"xg{a}", align_bytes=64) for a in range(PASSES)]
+        x_codes = [keep.tile([P, S], U32, name=f"xc{a}", align_bytes=64) for a in range(PASSES)]
+        x_scales = [keep.tile([P, S], U8, name=f"xs{a}", align_bytes=64) for a in range(PASSES)]
         acc = [
             [(psum.tile([P, n1 - n0], F32, name=f"acc{m}_{n0}"), n0, n1) for n0, n1 in cuts]
             for m, cuts in enumerate(CUTS)
@@ -81,76 +85,60 @@ def tile_list_heads_tm_hl_gelu_kernel(tc, xT, w, wgt, b, offs, out):
                     return tile[:, :, n0 - lo : n1 - lo]
             raise ValueError("columns of two loads")
 
-        for q in range(3):
-            load_w(0, q)
-        load_plane(0, 0)
-        nc.sync.dma_start(out=weights[:], in_=wgt)
-        nc.sync.dma_start(offsets[:], offs)
-        load_plane(0, 1)
-        load_plane(0, 2)
-        load_w(1, 0)
-        load_plane(0, 3)
-        for i in range(PACK):
-            load_plane(1, i)
-        nc.sync.dma_start(out=bias[:], in_=b.partition_broadcast(P))
-
         def gather(a, i, t0, t1):
-            h, cols = t0 // HALF, slice(t0 % HALF, t0 % HALF + t1 - t0)
             nc.vector.tensor_tensor(
-                picked[a][h][:, i, cols],
+                picked[a, t0 // 256][:, i, t0 % 256 : t0 % 256 + t1 - t0],
                 planes[a][i][:].indirect(offsets[:, t0 // 16 : t1 // 16]),
                 weights[:, t0:t1],
                 ALU.mult,
             )
 
-        def interleave(a, t0, t1):
-            h, cols = t0 // HALF, slice(t0 % HALF, t0 % HALF + t1 - t0)
-            nc.scalar.copy(packed(xg[a][h][:, cols, :]), four_by_four(picked[a][h][:, :, cols]))
+        def interleave(a, t0, t1, copy=nc.scalar.copy):
+            copy(packed(xg[a][:, t0:t1, :]), four_by_four(picked[a, t0 // 256][:, :, t0 % 256 : t0 % 256 + t1 - t0]))
 
         def quantize_x(a, t0, t1):
-            h, cols = t0 // HALF, slice(t0 % HALF, t0 % HALF + t1 - t0)
             nc.vector.quantize_mx(
-                out=x_codes[a][h][:, cols].bitcast(FP8X4),
-                scales=x_scales[a][h][:, cols],
-                in_=xg[a][h][:, cols, :].rearrange("p t j -> p (t j)"),
+                out=x_codes[a][:, t0:t1].bitcast(FP8X4),
+                scales=x_scales[a][:, t0:t1],
+                in_=xg[a][:, t0:t1, :].rearrange("p t j -> p (t j)"),
             )
 
-        def truncate(a, n0, n1, copy):
+        def truncate(a, n0, n1, copy=nc.scalar.copy):
             top = w_part(a, n0, n1).bitcast(BF16).rearrange("p j (n e) -> p j n e", e=2)[:, :, :, 1]
-            copy(packed(w_hi[a][:, n0:n1, :]), four_by_four(top))
+            copy(packed(split[a][:, HI, n0:n1, :]), four_by_four(top))
 
         def mask(a, n0, n1):
-            words = w_hi[a][:, n0:n1, :].rearrange("p n j -> p (n j)").bitcast(I32)
+            words = split[a][:, HI, n0:n1, :].rearrange("p n j -> p (n j)").bitcast(I32)
             nc.vector.tensor_scalar(words, words, HI_MASK, None, ALU.bitwise_and)
 
         def rest(a, n0, n1):
             nc.vector.tensor_tensor(
-                packed(w_lo[a][:, n0:n1, :]),
+                packed(split[a][:, LO, n0:n1, :]),
                 four_by_four(w_part(a, n0, n1)),
-                packed(w_hi[a][:, n0:n1, :]),
+                packed(split[a][:, HI, n0:n1, :]),
                 ALU.subtract,
             )
 
-        def quantize_w(codes, scales, source):
+        def quantize_w(a, first, last):
             nc.vector.quantize_mx(
-                out=codes[:].bitcast(FP8X4), scales=scales[:], in_=source[:].rearrange("p n j -> p (n j)")
+                out=w_codes[a][:, first : last + 1, :].rearrange("p h n -> p (h n)").bitcast(FP8X4),
+                scales=w_scales[a][:, first : last + 1, :].rearrange("p h n -> p (h n)"),
+                in_=split[a][:, first : last + 1, :, :].rearrange("p h n j -> p (h n j)"),
             )
 
-        def multiply(a, m, low):
-            h, cols = m // 2, slice((m % 2) * P, (m % 2) * P + P)
-            codes, scales = ((hi_codes[a], hi_scales[a]), (lo_codes[a], lo_scales[a]))[low]
+        def multiply(a, m, half):
             for bank, n0, n1 in acc[m]:
                 nc.tensor.matmul_mx(
                     out=bank[:],
-                    lhsT=x_codes[a][h][:, cols].bitcast(FP8X4),
-                    lhsT_scale=x_scales[a][h][:, cols],
-                    rhs=codes[:, n0:n1].bitcast(FP8X4),
-                    rhs_scale=scales[:, n0:n1],
-                    start=(a == 0 and low == 0),
-                    stop=(a == PASSES - 1 and low == 1),
+                    lhsT=x_codes[a][:, m * P : (m + 1) * P].bitcast(FP8X4),
+                    lhsT_scale=x_scales[a][:, m * P : (m + 1) * P],
+                    rhs=w_codes[a][:, half, n0:n1].bitcast(FP8X4),
+                    rhs_scale=w_scales[a][:, half, n0:n1],
+                    start=(a == 0 and half == HI),
+                    stop=(a == PASSES - 1 and half == LO),
                 )
 
-        def finish(m):
+        def finish(m, cuts=None):
             summed = keep.tile([P, M], F32, name=f"sum{m}")
             result = keep.tile([P, M], F32, name=f"res{m}")
             for bank, n0, n1 in acc[m]:
@@ -158,57 +146,75 @@ def tile_list_heads_tm_hl_gelu_kernel(tc, xT, w, wgt, b, offs, out):
                 nc.scalar.activation(result[:, n0:n1], summed[:, n0:n1], ACT.Gelu_apprx_tanh)
                 nc.sync.dma_start(out=out[m * P : (m + 1) * P, n0:n1], in_=result[:, n0:n1])
 
-        truncate(0, 0, 128, nc.vector.tensor_copy)
-        for n0 in range(0, M, 128):
-            if n0:
-                truncate(0, n0, n0 + 128, nc.scalar.copy)
-            mask(0, n0, n0 + 128)
-            rest(0, n0, n0 + 128)
-        quantize_w(hi_codes[0], hi_scales[0], w_hi[0])
-        for i in range(3):
+        for q in range(3):
+            load_w(0, q)
+        nc.sync.dma_start(out=weights[:], in_=wgt)
+        nc.sync.dma_start(offsets[:], offs)
+        load_plane(0, 0)
+        load_plane(0, 1)
+        load_w(1, 0)
+        load_plane(0, 2)
+        load_plane(0, 3)
+        for i in range(PACK):
+            load_plane(1, i)
+        nc.sync.dma_start(out=bias[:], in_=b.partition_broadcast(P))
+
+        truncate(0, 0, 128)
+        truncate(0, 128, 256, nc.vector.tensor_copy)
+        truncate(0, 256, 384)
+        truncate(0, 384, 512)
+        mask(0, 0, 128)
+        mask(0, 128, 256)
+        rest(0, 0, 128)
+        rest(0, 128, 256)
+        mask(0, 256, 384)
+        rest(0, 256, 384)
+        gather(0, 0, 0, 256)
+        mask(0, 384, 512)
+        gather(0, 0, 256, 512)
+        rest(0, 384, 512)
+        gather(0, 1, 0, 256)
+        gather(0, 1, 256, 512)
+        quantize_w(0, HI, LO)
+        for n0 in (0, 256):
+            truncate(1, n0, n0 + 256)
+        for i in (2, 3):
             gather(0, i, 0, 256)
             gather(0, i, 256, 512)
-        quantize_w(lo_codes[0], lo_scales[0], w_lo[0])
-        for n0 in (0, 256):
-            truncate(1, n0, n0 + 256, nc.scalar.copy)
-        mask(1, 0, 256)
-        gather(0, 3, 0, 256)
-        gather(0, 3, 256, 512)
+        mask(1, 0, 512)
+        gather(1, 0, 0, 256)
         interleave(0, 0, 256)
         interleave(0, 256, 512)
-        rest(1, 0, 256)
-        gather(1, 0, 0, 256)
-        mask(1, 256, 512)
-        quantize_x(0, 0, 256)
+        rest(1, 0, 512)
         gather(1, 1, 0, 256)
-        quantize_x(0, 256, 512)
-        for low in range(2):
-            for m in range(4):
-                multiply(0, m, low)
-        rest(1, 256, 512)
+        quantize_x(0, 0, 512)
+        for m in range(3):
+            multiply(0, m, HI)
+            multiply(0, m, LO)
+        multiply(0, 3, HI)
         gather(1, 2, 0, 256)
+        quantize_w(1, HI, LO)
+        picked[1, 1] = keep.tile([P, PACK, 256], F32, name="g11", tag="shared", align_bytes=64)
         gather(1, 3, 0, 256)
         interleave(1, 0, 256)
-        quantize_w(hi_codes[1], hi_scales[1], w_hi[1])
-        gather(1, 0, 256, 384)
         quantize_x(1, 0, 256)
-        quantize_w(lo_codes[1], lo_scales[1], w_lo[1])
         for m in range(2):
-            multiply(1, m, 0)
-            multiply(1, m, 1)
-        for i in range(1, PACK):
+            multiply(1, m, HI)
+            multiply(1, m, LO)
+        multiply(0, 3, LO)
+        for i in range(PACK):
             gather(1, i, 256, 384)
         interleave(1, 256, 384)
         for i in range(PACK):
             gather(1, i, 384, 512)
         interleave(1, 384, 512)
         quantize_x(1, 256, 384)
-        multiply(1, 2, 0)
-        multiply(1, 2, 1)
+        multiply(1, 2, HI)
+        multiply(1, 2, LO)
         finish(0)
         quantize_x(1, 384, 512)
-        multiply(1, 3, 0)
-        multiply(1, 3, 1)
         finish(1)
+        multiply(1, 3, HI)
+        multiply(1, 3, LO)
         finish(2)
         finish(3)

@@ -19,9 +19,10 @@ P = 128
 PACK = 4
 PASSES = K // (P * PACK)
 HI, LO = 0, 1
-LOADS = (((0, 128), (128, 256), (256, 512)), ((0, 512),))
+LOADS = (((0, 128), (128, 256), (256, 512)), ((0, 256), (256, 512)))
 CUTS = (((0, 512),), ((0, 512),), ((0, 512),), ((0, 256), (256, 512)))
 HI_MASK = -0x000F0010
+CUT_MASK = -0x00100000
 
 
 def four_by_four(view):
@@ -51,12 +52,13 @@ def tile_list_heads_tm_hl_gelu_kernel(tc, xT, w, wgt, b, offs, out):
             keep.tile([P, 2, M, PACK], BF16, name="split0", align_bytes=64),
             keep.tile([P, 2, M, PACK], BF16, name="split1", tag="shared", align_bytes=64),
         ]
+        w_top = keep.tile([P, PACK, M], F32, name="w_top")
         w_codes = [keep.tile([P, 2, M], U32, name=f"wc{a}", align_bytes=64) for a in range(PASSES)]
         w_scales = [keep.tile([P, 2, M], U8, name=f"ws{a}", align_bytes=64) for a in range(PASSES)]
         picked = {
-            (0, 0): keep.tile([P, PACK, 256], F32, name="g00"),
-            (0, 1): keep.tile([P, PACK, 256], F32, name="g01"),
-            (1, 0): keep.tile([P, PACK, 256], F32, name="g10"),
+            (0, 0): keep.tile([P, PACK, 256], F32, name="g0_0"),
+            (0, 256): keep.tile([P, PACK, 256], F32, name="g0_256"),
+            (1, 0): keep.tile([P, PACK, 256], F32, name="g1_0", tag="front", align_bytes=64),
         }
         xg = [keep.tile([P, S, PACK], BF16, name=f"xg{a}", align_bytes=64) for a in range(PASSES)]
         x_codes = [keep.tile([P, S], U32, name=f"xc{a}", align_bytes=64) for a in range(PASSES)]
@@ -87,14 +89,14 @@ def tile_list_heads_tm_hl_gelu_kernel(tc, xT, w, wgt, b, offs, out):
 
         def gather(a, i, t0, t1):
             nc.vector.tensor_tensor(
-                picked[a, t0 // 256][:, i, t0 % 256 : t0 % 256 + t1 - t0],
+                picked[a, t0][:, i, :],
                 planes[a][i][:].indirect(offsets[:, t0 // 16 : t1 // 16]),
                 weights[:, t0:t1],
                 ALU.mult,
             )
 
         def interleave(a, t0, t1, copy=nc.scalar.copy):
-            copy(packed(xg[a][:, t0:t1, :]), four_by_four(picked[a, t0 // 256][:, :, t0 % 256 : t0 % 256 + t1 - t0]))
+            copy(packed(xg[a][:, t0:t1, :]), four_by_four(picked[a, t0][:]))
 
         def quantize_x(a, t0, t1):
             nc.vector.quantize_mx(
@@ -110,6 +112,22 @@ def tile_list_heads_tm_hl_gelu_kernel(tc, xT, w, wgt, b, offs, out):
         def mask(a, n0, n1):
             words = split[a][:, HI, n0:n1, :].rearrange("p n j -> p (n j)").bitcast(I32)
             nc.vector.tensor_scalar(words, words, HI_MASK, None, ALU.bitwise_and)
+
+        def cut(n0, n1):
+            nc.vector.tensor_scalar(
+                w_top[:, :, n0:n1].bitcast(I32), w_part(0, n0, n1).bitcast(I32), CUT_MASK, None, ALU.bitwise_and
+            )
+
+        def round_cut(n0, n1):
+            nc.scalar.copy(packed(split[0][:, HI, n0:n1, :]), four_by_four(w_top[:, :, n0:n1]))
+
+        def rest_of_cut(n0, n1):
+            nc.vector.tensor_tensor(
+                packed(split[0][:, LO, n0:n1, :]),
+                four_by_four(w_part(0, n0, n1)),
+                four_by_four(w_top[:, :, n0:n1]),
+                ALU.subtract,
+            )
 
         def rest(a, n0, n1):
             nc.vector.tensor_tensor(
@@ -152,41 +170,43 @@ def tile_list_heads_tm_hl_gelu_kernel(tc, xT, w, wgt, b, offs, out):
         nc.sync.dma_start(offsets[:], offs)
         load_plane(0, 0)
         load_plane(0, 1)
-        load_w(1, 0)
         load_plane(0, 2)
+        load_w(1, 0)
         load_plane(0, 3)
+        load_w(1, 1)
         for i in range(PACK):
             load_plane(1, i)
         nc.sync.dma_start(out=bias[:], in_=b.partition_broadcast(P))
 
-        truncate(0, 0, 128)
-        truncate(0, 128, 256, nc.vector.tensor_copy)
-        truncate(0, 256, 384)
-        truncate(0, 384, 512)
-        mask(0, 0, 128)
-        mask(0, 128, 256)
-        rest(0, 0, 128)
-        rest(0, 128, 256)
-        mask(0, 256, 384)
-        rest(0, 256, 384)
+        for n0 in (0, 128):
+            cut(n0, n0 + 128)
+            round_cut(n0, n0 + 128)
+        rest_of_cut(0, 128)
+        rest_of_cut(128, 256)
+        for n0 in (256, 384):
+            cut(n0, n0 + 128)
+            round_cut(n0, n0 + 128)
+        rest_of_cut(256, 384)
+        rest_of_cut(384, 512)
         gather(0, 0, 0, 256)
-        mask(0, 384, 512)
         gather(0, 0, 256, 512)
-        rest(0, 384, 512)
         gather(0, 1, 0, 256)
         gather(0, 1, 256, 512)
         quantize_w(0, HI, LO)
-        for n0 in (0, 256):
-            truncate(1, n0, n0 + 256)
-        for i in (2, 3):
-            gather(0, i, 0, 256)
-            gather(0, i, 256, 512)
-        mask(1, 0, 512)
-        gather(1, 0, 0, 256)
+        truncate(1, 0, 256)
+        gather(0, 2, 0, 256)
+        mask(1, 0, 256)
+        gather(0, 2, 256, 512)
+        rest(1, 0, 256)
+        gather(0, 3, 0, 256)
+        gather(0, 3, 256, 512)
         interleave(0, 0, 256)
+        truncate(1, 256, 512)
         interleave(0, 256, 512)
-        rest(1, 0, 512)
+        gather(1, 0, 0, 256)
+        mask(1, 256, 512)
         gather(1, 1, 0, 256)
+        rest(1, 256, 512)
         quantize_x(0, 0, 512)
         for m in range(3):
             multiply(0, m, HI)
@@ -194,7 +214,7 @@ def tile_list_heads_tm_hl_gelu_kernel(tc, xT, w, wgt, b, offs, out):
         multiply(0, 3, HI)
         gather(1, 2, 0, 256)
         quantize_w(1, HI, LO)
-        picked[1, 1] = keep.tile([P, PACK, 256], F32, name="g11", tag="shared", align_bytes=64)
+        picked[1, 256] = keep.tile([P, PACK, 128], F32, name="g1_256", tag="shared", align_bytes=64)
         gather(1, 3, 0, 256)
         interleave(1, 0, 256)
         quantize_x(1, 0, 256)
@@ -205,6 +225,7 @@ def tile_list_heads_tm_hl_gelu_kernel(tc, xT, w, wgt, b, offs, out):
         for i in range(PACK):
             gather(1, i, 256, 384)
         interleave(1, 256, 384)
+        picked[1, 384] = keep.tile([P, PACK, 128], F32, name="g1_384", tag="front", align_bytes=64)
         for i in range(PACK):
             gather(1, i, 384, 512)
         interleave(1, 384, 512)

from contextlib import ExitStack

import concourse.mybir as mybir

K, M, T, S = 1024, 512, 1024, 512
FLOPS = 2 * 2 * K * M * S

F32 = mybir.dt.float32
BF16 = mybir.dt.bfloat16
I32 = mybir.dt.int32
U32 = mybir.dt.uint32
U16 = mybir.dt.uint16
U8 = mybir.dt.uint8
FP8X4 = mybir.dt.float8_e4m3fn_x4
ALU = mybir.AluOpType
ACT = mybir.ActivationFunctionType

P = 128
PACK = 4
PASSES = K // (P * PACK)
HI, LO = 0, 1
LOADS = (((0, 128), (128, 256), (256, 512)), ((0, 256), (256, 512)))
CUTS = (((0, 512),), ((0, 512),), ((0, 512),), ((0, 256), (256, 512)))
HI_MASK = -0x000F0010
CUT_MASK = -0x00100000


def four_by_four(view):
    return view.rearrange("p j (c i) -> p c j i", i=4)


def packed(view):
    return view.rearrange("p (c i) j -> p c j i", i=4)


def tile_list_heads_tm_hl_gelu_kernel(tc, xT, w, wgt, b, offs, out):
    nc = tc.nc
    with ExitStack() as ctx:
        keep = ctx.enter_context(tc.tile_pool(name="keep", bufs=1))
        psum = ctx.enter_context(tc.psum_pool(name="psum", bufs=1))

        offsets = keep.tile([P, S // 16], U16, name="offsets")
        weights = keep.tile([P, S], F32, name="weights")
        bias = keep.tile([P, M], F32, name="bias")
        warm = keep.tile([P, 2], F32, name="warm")
        planes = [[keep.tile([P, T], F32, name=f"x{a}{i}") for i in range(PACK)] for a in range(PASSES)]
        w_raw = [
            [(keep.tile([P, PACK, n1 - n0], F32, name=f"w{a}_{n0}"), n0, n1) for n0, n1 in LOADS[a]]
            for a in range(PASSES)
        ]
        split = [
            keep.tile([P, 2, M, PACK], BF16, name="split0", align_bytes=64),
            keep.tile([P, 2, M, PACK], BF16, name="split1", tag="shared", align_bytes=64),
        ]
        w_top = keep.tile([P, PACK, M], F32, name="w_top")
        w_codes = [keep.tile([P, 2, M], U32, name=f"wc{a}", align_bytes=64) for a in range(PASSES)]
        w_scales = [keep.tile([P, 2, M], U8, name=f"ws{a}", align_bytes=64) for a in range(PASSES)]
        picked = {
            (0, 0): keep.tile([P, PACK, 256], F32, name="g0_0"),
            (0, 256): keep.tile([P, PACK, 256], F32, name="g0_256"),
            (1, 0): keep.tile([P, PACK, 256], F32, name="g1_0", tag="front", align_bytes=64),
        }
        xg = [keep.tile([P, S, PACK], BF16, name=f"xg{a}", align_bytes=64) for a in range(PASSES)]
        x_codes = [keep.tile([P, S], U32, name=f"xc{a}", align_bytes=64) for a in range(PASSES)]
        x_scales = [keep.tile([P, S], U8, name=f"xs{a}", align_bytes=64) for a in range(PASSES)]
        acc = [
            [(psum.tile([P, n1 - n0], F32, name=f"acc{m}_{n0}"), n0, n1) for n0, n1 in cuts]
            for m, cuts in enumerate(CUTS)
        ]

        xv = xT.rearrange("(a p j) t -> a j p t", a=PASSES, j=PACK)
        wv = w.rearrange("(a p j) n -> a p j n", a=PASSES, j=PACK)

        nc.gpsimd.memset(warm[:, 0:1], 0.0)
        nc.scalar.activation(warm[:, 1:2], warm[:, 0:1], ACT.Gelu_apprx_tanh)

        def load_plane(a, i):
            nc.sync.dma_start(out=planes[a][i][:], in_=xv[a, i])

        def load_w(a, q):
            tile, n0, n1 = w_raw[a][q]
            nc.sync.dma_start(out=tile[:], in_=wv[a, :, :, n0:n1])

        def w_part(a, n0, n1):
            for tile, lo, hi in w_raw[a]:
                if lo <= n0 and n1 <= hi:
                    return tile[:, :, n0 - lo : n1 - lo]
            raise ValueError("columns of two loads")

        def gather(a, i, t0, t1):
            nc.vector.tensor_tensor(
                picked[a, t0][:, i, :],
                planes[a][i][:].indirect(offsets[:, t0 // 16 : t1 // 16]),
                weights[:, t0:t1],
                ALU.mult,
            )

        def interleave(a, t0, t1, copy=nc.scalar.copy):
            copy(packed(xg[a][:, t0:t1, :]), four_by_four(picked[a, t0][:]))

        def quantize_x(a, t0, t1):
            nc.vector.quantize_mx(
                out=x_codes[a][:, t0:t1].bitcast(FP8X4),
                scales=x_scales[a][:, t0:t1],
                in_=xg[a][:, t0:t1, :].rearrange("p t j -> p (t j)"),
            )

        def truncate(a, n0, n1, copy=nc.scalar.copy):
            top = w_part(a, n0, n1).bitcast(BF16).rearrange("p j (n e) -> p j n e", e=2)[:, :, :, 1]
            copy(packed(split[a][:, HI, n0:n1, :]), four_by_four(top))

        def mask(a, n0, n1):
            words = split[a][:, HI, n0:n1, :].rearrange("p n j -> p (n j)").bitcast(I32)
            nc.vector.tensor_scalar(words, words, HI_MASK, None, ALU.bitwise_and)

        def cut(n0, n1):
            nc.vector.tensor_scalar(
                w_top[:, :, n0:n1].bitcast(I32), w_part(0, n0, n1).bitcast(I32), CUT_MASK, None, ALU.bitwise_and
            )

        def round_cut(n0, n1):
            nc.scalar.copy(packed(split[0][:, HI, n0:n1, :]), four_by_four(w_top[:, :, n0:n1]))

        def rest_of_cut(n0, n1):
            nc.vector.tensor_tensor(
                packed(split[0][:, LO, n0:n1, :]),
                four_by_four(w_part(0, n0, n1)),
                four_by_four(w_top[:, :, n0:n1]),
                ALU.subtract,
            )

        def rest(a, n0, n1):
            nc.vector.tensor_tensor(
                packed(split[a][:, LO, n0:n1, :]),
                four_by_four(w_part(a, n0, n1)),
                packed(split[a][:, HI, n0:n1, :]),
                ALU.subtract,
            )

        def quantize_w(a, first, last):
            nc.vector.quantize_mx(
                out=w_codes[a][:, first : last + 1, :].rearrange("p h n -> p (h n)").bitcast(FP8X4),
                scales=w_scales[a][:, first : last + 1, :].rearrange("p h n -> p (h n)"),
                in_=split[a][:, first : last + 1, :, :].rearrange("p h n j -> p (h n j)"),
            )

        def multiply(a, m, half):
            for bank, n0, n1 in acc[m]:
                nc.tensor.matmul_mx(
                    out=bank[:],
                    lhsT=x_codes[a][:, m * P : (m + 1) * P].bitcast(FP8X4),
                    lhsT_scale=x_scales[a][:, m * P : (m + 1) * P],
                    rhs=w_codes[a][:, half, n0:n1].bitcast(FP8X4),
                    rhs_scale=w_scales[a][:, half, n0:n1],
                    start=(a == 0 and half == HI),
                    stop=(a == PASSES - 1 and half == LO),
                )

        def finish(m, cuts=None):
            summed = keep.tile([P, M], F32, name=f"sum{m}")
            result = keep.tile([P, M], F32, name=f"res{m}")
            for bank, n0, n1 in acc[m]:
                nc.vector.tensor_tensor(summed[:, n0:n1], bank[:], bias[:, n0:n1], ALU.add)
                nc.scalar.activation(result[:, n0:n1], summed[:, n0:n1], ACT.Gelu_apprx_tanh)
                nc.sync.dma_start(out=out[m * P : (m + 1) * P, n0:n1], in_=result[:, n0:n1])

        for q in range(3):
            load_w(0, q)
        nc.sync.dma_start(out=weights[:], in_=wgt)
        nc.sync.dma_start(offsets[:], offs)
        load_plane(0, 0)
        load_plane(0, 1)
        load_plane(0, 2)
        load_w(1, 0)
        load_plane(0, 3)
        load_w(1, 1)
        for i in range(PACK):
            load_plane(1, i)
        nc.sync.dma_start(out=bias[:], in_=b.partition_broadcast(P))

        for n0 in (0, 128):
            cut(n0, n0 + 128)
            round_cut(n0, n0 + 128)
        rest_of_cut(0, 128)
        rest_of_cut(128, 256)
        for n0 in (256, 384):
            cut(n0, n0 + 128)
            round_cut(n0, n0 + 128)
        rest_of_cut(256, 384)
        rest_of_cut(384, 512)
        gather(0, 0, 0, 256)
        gather(0, 0, 256, 512)
        gather(0, 1, 0, 256)
        gather(0, 1, 256, 512)
        quantize_w(0, HI, LO)
        truncate(1, 0, 256)
        gather(0, 2, 0, 256)
        mask(1, 0, 256)
        gather(0, 2, 256, 512)
        rest(1, 0, 256)
        gather(0, 3, 0, 256)
        gather(0, 3, 256, 512)
        interleave(0, 0, 256)
        truncate(1, 256, 512)
        interleave(0, 256, 512)
        gather(1, 0, 0, 256)
        mask(1, 256, 512)
        gather(1, 1, 0, 256)
        rest(1, 256, 512)
        quantize_x(0, 0, 512)
        for m in range(3):
            multiply(0, m, HI)
            multiply(0, m, LO)
        multiply(0, 3, HI)
        gather(1, 2, 0, 256)
        quantize_w(1, HI, LO)
        picked[1, 256] = keep.tile([P, PACK, 128], F32, name="g1_256", tag="shared", align_bytes=64)
        gather(1, 3, 0, 256)
        interleave(1, 0, 256)
        quantize_x(1, 0, 256)
        for m in range(2):
            multiply(1, m, HI)
            multiply(1, m, LO)
        multiply(0, 3, LO)
        for i in range(PACK):
            gather(1, i, 256, 384)
        interleave(1, 256, 384)
        picked[1, 384] = keep.tile([P, PACK, 128], F32, name="g1_384", tag="front", align_bytes=64)
        for i in range(PACK):
            gather(1, i, 384, 512)
        interleave(1, 384, 512)
        quantize_x(1, 256, 384)
        multiply(1, 2, HI)
        multiply(1, 2, LO)
        finish(0)
        quantize_x(1, 384, 512)
        finish(1)
        multiply(1, 3, HI)
        multiply(1, 3, LO)
        finish(2)
        finish(3)
